import numpy as np
import ml_dtypes


def mxq(x, axis, fmt="e4m3"):
    dtype, down = {"e4m3": (ml_dtypes.float8_e4m3fn, 7), "e5m2": (ml_dtypes.float8_e5m2, 14)}[fmt]
    v = np.moveaxis(np.asarray(x, np.float32).astype(ml_dtypes.bfloat16).astype(np.float64), axis, -1)
    blocks = v.reshape(v.shape[:-1] + (-1, 32))
    amax = np.abs(blocks).max(-1, keepdims=True)
    byte = np.maximum(np.where(amax > 0, np.frexp(amax)[1] - 1 + 127, 0) - down, 1)
    scale = np.exp2(byte - 127.0)
    codes = (blocks / scale).astype(np.float32).astype(dtype).astype(np.float64)
    return np.moveaxis((codes * scale).reshape(v.shape), -1, axis)


WIDE = False


def mx_kscale(k):
    if not WIDE:
        return np.ones(k)
    levels = np.array([10, -10, 5, -5, 0])
    if k % 512:
        return np.exp2(np.random.permutation(np.resize(levels, k // 32))).repeat(32)
    a = np.empty((k // 512, 16))
    for p in range(k // 512):
        a[p, :8] = np.random.permutation(np.resize(levels, 8))
        for g in range(8):
            far = levels[np.abs(levels - a[p, g]) >= 10]
            a[p, g + 8] = far[np.random.randint(len(far))]
    return np.exp2(a.ravel()).repeat(32)


def f64(x):
    return np.asarray(x).astype(np.float64)


def striped(idx):
    return np.tile(idx.reshape(-1, 16).T, (8, 1)).astype(np.uint16)


def unstriped(offs):
    return offs[:16].T.reshape(-1).astype(np.int64)


def pack_weight(w):
    k, n = w.shape
    w = f64(np.asarray(w, np.float32).astype(ml_dtypes.bfloat16)).reshape(k // 32, 32, n)
    amax = np.abs(w).max(1)
    byte = np.clip(np.where(amax > 0, np.frexp(amax)[1] - 1 + 127 - 7, 1), 1, 254)
    scaled = (w * np.exp2(127.0 - byte)[:, None, :]).reshape(k, n).astype(np.float32)
    words = np.ascontiguousarray(scaled.reshape(k // 512, 128, 4, n).transpose(0, 1, 3, 2)).astype(ml_dtypes.float8_e4m3fn).view(np.uint8)
    return words, np.ascontiguousarray(byte.astype(np.uint8).reshape(k // 512, 16, n))


def unpack_weight(words, scales):
    g, p, n, _ = words.shape
    vals = np.ascontiguousarray(words).view(ml_dtypes.float8_e4m3fn).astype(np.float64) * np.repeat(np.exp2(scales.astype(np.float64) - 127.0), 8, axis=1)[..., None]
    return vals.transpose(0, 1, 3, 2).reshape(g * 512, n)


K, T, S, V = 1024, 2048, 512, 256
P = 2 ** 7


def setup_inputs():
    n = np.random.standard_normal
    s = mx_kscale(K)[:, None]
    packed_xT = pack_weight(n((K, T)) * s)
    return {
        "x_words": packed_xT[0],
        "x_scales": packed_xT[1],
        "hT": (n((K, V)) / np.sqrt(K) / s).astype(np.float32),
        "eo": (np.tile(-np.random.uniform(0.5, 2.0, S), (P, 1))).astype(np.float32),
        "ev": (-np.random.uniform(0.3, 1.5, (V, 1))).astype(np.float32),
        "offs": striped(np.random.permutation(T)[:S]),
        "swp": striped(np.random.permutation(S)),
    }


def reference(x_words, x_scales, hT, eo, ev, offs, swp):
    hTq = mxq(f64(hT), 0, "e4m3")
    xq = unpack_weight(x_words, x_scales)[:, unstriped(offs)]
    y = hTq.T @ xq
    yx = y[:, unstriped(swp)]
    den = f64(eo)[:1] + f64(ev)
    reg = -1.0 * np.exp(0.7 * den) + 1.0
    return ((y * (2.0 * y - yx)) * ((reg) ** 2)) / den

@@ -1,0 +1,160 @@
+from contextlib import ExitStack
+
+import concourse.mybir as mybir
+from concourse.masks import make_identity
+
+K, T, S, V = 1024, 2048, 512, 256
+FLOPS = 2 * K * S * V
+BYTES = K * T + K // 32 * T + 4 * K * V + 4 * S + 4 * V + 2 * 2 * 128 * (S // 16) + 4 * V * S
+
+F32 = mybir.dt.float32
+BF16 = mybir.dt.bfloat16
+I32 = mybir.dt.int32
+U32 = mybir.dt.uint32
+U16 = mybir.dt.uint16
+U8 = mybir.dt.uint8
+FP8X4 = mybir.dt.float8_e4m3fn_x4
+ALU = mybir.AluOpType
+ACT = mybir.ActivationFunctionType
+
+P = 128
+PACK = 4
+PASSES = K // (P * PACK)
+BLOCKS = V // P
+HALF = S // 2
+LANES = 16
+QUAD = 32
+RATE = 0.7
+EXP_FLOOR = 1e-18
+
+
+def tile_picked_ymp2_reg_p_kernel(tc, x_words, x_scales, hT, eo, ev, offs, swp, out):
+    nc = tc.nc
+    with ExitStack() as ctx:
+        sb = ctx.enter_context(tc.tile_pool(name="sb", bufs=1))
+        ps = ctx.enter_context(tc.psum_pool(name="ps", bufs=1))
+
+        offs_sb = sb.tile([P, S // LANES], U16, name="offs_sb")
+        swp_sb = sb.tile([P, S // LANES], U16, name="swp_sb")
+        eo_col = sb.tile([P, PACK], F32, name="eo_col")
+        ev_col = sb.tile([P, BLOCKS], F32, name="ev_col")
+        h_raw = [sb.tile([P, PACK, V], F32, name=f"h_raw{a}") for a in range(PASSES)]
+        words = [sb.tile([P, T], U32, name=f"words{a}") for a in range(PASSES)]
+        scale_rows = sb.tile([P, T], U8, name="scale_rows", tag="scales_then_picked", align_bytes=64)
+
+        nc.scalar.dma_start(eo_col[:], eo[0:1, :].rearrange("o (p c) -> (o p) c", c=PACK))
+        nc.scalar.dma_start(ev_col[:], ev.rearrange("(p b) o -> p (b o)", b=BLOCKS))
+        h_rows = hT.rearrange("(a p j) w -> a p j w", a=PASSES, j=PACK)
+        nc.sync.dma_start(h_raw[0][:], h_rows[0])
+        nc.sync.dma_start(offs_sb[:], offs)
+        nc.sync.dma_start(h_raw[1][:], h_rows[1])
+        for a in range(PASSES):
+            nc.sync.dma_start(words[a][:].bitcast(I32), x_words[a].rearrange("p n t -> p (n t)").bitcast(I32))
+        nc.sync.dma_start(swp_sb[:], swp)
+
+        nc.vector.memset(scale_rows[:].bitcast(I32), 0)
+        ident = sb.tile([P, P], F32, name="ident")
+        make_identity(nc, ident[:])
+        for q in range(P // QUAD):
+            nc.gpsimd.dma_start(
+                scale_rows[:].bitcast(I32)[QUAD * q : QUAD * q + PACK * PASSES, :],
+                x_scales.bitcast(I32)[:, PACK * q : PACK * (q + 1), :],
+            )
+
+        exp_eo = sb.tile([P, PACK], F32, name="exp_eo")
+        nc.scalar.activation(exp_eo[:], eo_col[:], ACT.Exp, scale=RATE)
+        exp_ev_raw = sb.tile([P, BLOCKS], F32, name="exp_ev_raw")
+        nc.scalar.activation(exp_ev_raw[:], ev_col[:], ACT.Exp, scale=RATE)
+        exp_ev = sb.tile([P, BLOCKS], F32, name="exp_ev")
+        nc.vector.tensor_scalar_max(exp_ev[:], exp_ev_raw[:], EXP_FLOOR)
+        inv_exp_ev = sb.tile([P, BLOCKS], F32, name="inv_exp_ev")
+        nc.vector.reciprocal(inv_exp_ev[:], exp_ev[:])
+
+        eo_ps = ps.tile([P, PACK, P], F32, name="eo_ps", tag="bank00")
+        for c in range(PACK):
+            nc.tensor.transpose(eo_ps[:, c, :], eo_col[:, c : c + 1].to_broadcast([P, P]), ident[:])
+        exp_ps = ps.tile([P, PACK, P], F32, name="exp_ps", tag="bank10")
+        for c in range(PACK):
+            nc.tensor.transpose(exp_ps[:, c, :], exp_eo[:, c : c + 1].to_broadcast([P, P]), ident[:])
+
+        rs = []
+        for b in range(BLOCKS):
+            r = sb.tile([P, P, PACK], F32, name=f"rsq{b}", tag=f"rsq{b}", align_bytes=64)
+            nc.scalar.activation(r[:], eo_ps[:].rearrange("p c n -> p n c"), ACT.Abs_reciprocal_sqrt, bias=ev_col[:, b : b + 1])
+            rs.append(r)
+
+        picked_scales = sb.tile([P, S], U8, name="picked_scales", align_bytes=64)
+        nc.vector.tensor_copy(picked_scales[:], scale_rows[:].indirect(offs_sb[:]))
+
+        ms = []
+        for b in range(BLOCKS):
+            m = sb.tile([P, P, PACK], F32, name=f"root{b}", tag=f"root{b}")
+            nc.vector.scalar_tensor_tensor(
+                m[:], exp_ps[:].rearrange("p c n -> p n c"), inv_exp_ev[:, b : b + 1], rs[b][:], ALU.subtract, ALU.mult
+            )
+            ms.append(m)
+
+        h_codes, h_scales = [], []
+        for a in range(PASSES):
+            grouped = sb.tile([P, V * PACK], BF16, name=f"grouped{a}", align_bytes=64)
+            (nc.vector.tensor_copy if a == 0 else nc.scalar.copy)(
+                grouped[:].rearrange("p (b c m j) -> p c j m b", b=BLOCKS, m=2, j=PACK),
+                h_raw[a][:].rearrange("p j (c m b) -> p c j m b", m=2, b=BLOCKS),
+            )
+            codes = sb.tile([P, V], U32, name=f"h_codes{a}", align_bytes=64)
+            scales = sb.tile([P, V], U8, name=f"h_scales{a}", align_bytes=64)
+            nc.vector.quantize_mx(out=codes[:].bitcast(FP8X4), scales=scales[:], in_=grouped[:])
+            h_codes.append(codes)
+            h_scales.append(scales)
+
+        neg_f = []
+        for b in range(BLOCKS):
+            f = sb.tile([P, S], F32, name=f"neg_f{b}")
+            nc.scalar.activation(f[:], ms[b][:].rearrange("p n c -> p (n c)"), ACT.Square, scale=exp_ev[:, b : b + 1])
+            neg_f.append(f)
+
+        y_ps = [[ps.tile([P, HALF], F32, name=f"y_ps{b}{h}", tag=f"bank{b}{h}") for h in range(2)] for b in range(BLOCKS)]
+
+        def product(a, h, picked):
+            for b in range(BLOCKS):
+                nc.tensor.matmul_mx(
+                    out=y_ps[b][h][:],
+                    lhsT=h_codes[a][:, P * b : P * (b + 1)].bitcast(FP8X4),
+                    lhsT_scale=h_scales[a][:, P * b : P * (b + 1)],
+                    rhs=picked.bitcast(FP8X4),
+                    rhs_scale=picked_scales[PACK * a :, HALF * h : HALF * (h + 1)],
+                    start=(a == 0),
+                    stop=(a == PASSES - 1),
+                )
+
+        picked0 = sb.tile([P, S], U32, name="picked0", tag="rsq1", align_bytes=64)
+        nc.vector.tensor_copy(picked0[:], words[0][:].indirect(offs_sb[:]))
+        for h in range(2):
+            product(0, h, picked0[:, HALF * h : HALF * (h + 1)])
+        cols = HALF // LANES
+        for h in range(2):
+            picked1 = sb.tile([P, HALF], U32, name=f"picked1{h}", tag=("scales_then_picked" if h == 0 else "picked_last"), align_bytes=64)
+            nc.vector.tensor_copy(picked1[:], words[1][:].indirect(offs_sb[:, cols * h : cols * (h + 1)]))
+            product(1, h, picked1[:])
+
+        y_sb = [sb.tile([P, S], F32, name=f"y_sb{b}", tag=f"root{1 - b}") for b in range(BLOCKS)]
+        yf = [[sb.tile([P, HALF], F32, name=f"yf{b}{h}") for h in range(2)] for b in range(BLOCKS)]
+        for h in range(2):
+            for b in range(BLOCKS):
+                if h == 1 and b == 1:
+                    nc.vector.tensor_copy(y_sb[b][:, HALF * h : HALF * (h + 1)], y_ps[b][h][:])
+                else:
+                    nc.scalar.copy(y_sb[b][:, HALF * h : HALF * (h + 1)], y_ps[b][h][:])
+            for b in range(BLOCKS):
+                nc.vector.tensor_tensor(yf[b][h][:], y_ps[b][h][:], neg_f[b][:, HALF * h : HALF * (h + 1)], ALU.mult)
+
+        out_rows = out.rearrange("(p b) n -> b p n", b=BLOCKS)
+        for b in range(BLOCKS):
+            for h in range(2):
+                yx = sb.tile([P, HALF], F32, name=f"yx{b}{h}")
+                nc.scalar.activation(yx[:], y_sb[b][:].indirect(swp_sb[:, cols * h : cols * (h + 1)]), ACT.Copy)
+                diff = sb.tile([P, HALF], F32, name=f"diff{b}{h}")
+                nc.vector.scalar_tensor_tensor(diff[:], y_ps[b][h][:], -2.0, yx[:], ALU.mult, ALU.add)
+                res = sb.tile([P, HALF], F32, name=f"res{b}{h}")
+                nc.vector.tensor_tensor(res[:], diff[:], yf[b][h][:], ALU.mult)
+                nc.sync.dma_start(out_rows[b][:, HALF * h : HALF * (h + 1)], res[:])

@@ -1,7 +1,6 @@
 from contextlib import ExitStack
 
 import concourse.mybir as mybir
-from concourse.masks import make_identity
 
 K, T, S, V = 1024, 2048, 512, 256
 FLOPS = 2 * K * S * V
@@ -36,27 +35,28 @@ def tile_picked_ymp2_reg_p_kernel(tc, x_words, x_scales, hT, eo, ev, offs, swp, 
 
         offs_sb = sb.tile([P, S // LANES], U16, name="offs_sb")
         swp_sb = sb.tile([P, S // LANES], U16, name="swp_sb")
-        eo_col = sb.tile([P, PACK], F32, name="eo_col")
-        ev_col = sb.tile([P, BLOCKS], F32, name="ev_col")
+        eo_col = sb.tile([P, PACK], F32, name="eo_col", tag="eo_then_words")
+        ev_col = sb.tile([P, BLOCKS], F32, name="ev_col", tag="grouped1", align_bytes=64)
         h_raw = [sb.tile([P, PACK, V], F32, name=f"h_raw{a}") for a in range(PASSES)]
-        words = [sb.tile([P, T], U32, name=f"words{a}") for a in range(PASSES)]
         scale_rows = sb.tile([P, T], U8, name="scale_rows", tag="scales_then_picked", align_bytes=64)
 
-        nc.scalar.dma_start(eo_col[:], eo[0:1, :].rearrange("o (p c) -> (o p) c", c=PACK))
-        nc.scalar.dma_start(ev_col[:], ev.rearrange("(p b) o -> p (b o)", b=BLOCKS))
-        h_rows = hT.rearrange("(a p j) w -> a p j w", a=PASSES, j=PACK)
-        nc.sync.dma_start(h_raw[0][:], h_rows[0])
-        nc.sync.dma_start(offs_sb[:], offs)
-        nc.sync.dma_start(h_raw[1][:], h_rows[1])
-        for a in range(PASSES):
-            nc.sync.dma_start(words[a][:].bitcast(I32), x_words[a].rearrange("p n t -> p (n t)").bitcast(I32))
-        nc.sync.dma_start(swp_sb[:], swp)
-
-        nc.vector.memset(scale_rows[:].bitcast(I32), 0)
+        nc.gpsimd.memset(scale_rows[:].bitcast(I32), 0)
+        zeros = sb.tile([P, P], F32, name="zeros", tag="zeros_then_words")
+        nc.gpsimd.memset(zeros[:], 0.0)
         ident = sb.tile([P, P], F32, name="ident")
-        make_identity(nc, ident[:])
+        nc.gpsimd.affine_select(
+            out=ident[:], in_=zeros[:], compare_op=ALU.not_equal, fill=1.0, base=0, pattern=[[-1, P]], channel_multiplier=1
+        )
+
+        nc.sync.dma_start(eo_col[:], eo[0:1, :].rearrange("o (p c) -> (o p) c", c=PACK))
+        nc.sync.dma_start(ev_col[:], ev.rearrange("(p b) o -> p (b o)", b=BLOCKS))
+        nc.sync.dma_start(offs_sb[:], offs)
+        nc.sync.dma_start(swp_sb[:], swp)
+        h_rows = hT.rearrange("(a p j) w -> a p j w", a=PASSES, j=PACK)
+        for a in range(PASSES):
+            nc.sync.dma_start(h_raw[a][:], h_rows[a])
         for q in range(P // QUAD):
-            nc.gpsimd.dma_start(
+            nc.sync.dma_start(
                 scale_rows[:].bitcast(I32)[QUAD * q : QUAD * q + PACK * PASSES, :],
                 x_scales.bitcast(I32)[:, PACK * q : PACK * (q + 1), :],
             )
@@ -77,6 +77,12 @@ def tile_picked_ymp2_reg_p_kernel(tc, x_words, x_scales, hT, eo, ev, offs, swp, 
         for c in range(PACK):
             nc.tensor.transpose(exp_ps[:, c, :], exp_eo[:, c : c + 1].to_broadcast([P, P]), ident[:])
 
+        words = []
+        for a, tag in enumerate(("zeros_then_words", "eo_then_words")):
+            w = sb.tile([P, T], U32, name=f"words{a}", tag=tag)
+            nc.sync.dma_start(w[:].bitcast(I32), x_words[a].rearrange("p n t -> p (n t)").bitcast(I32))
+            words.append(w)
+
         rs = []
         for b in range(BLOCKS):
             r = sb.tile([P, P, PACK], F32, name=f"rsq{b}", tag=f"rsq{b}", align_bytes=64)
@@ -96,7 +102,7 @@ def tile_picked_ymp2_reg_p_kernel(tc, x_words, x_scales, hT, eo, ev, offs, swp, 
 
         h_codes, h_scales = [], []
         for a in range(PASSES):
-            grouped = sb.tile([P, V * PACK], BF16, name=f"grouped{a}", align_bytes=64)
+            grouped = sb.tile([P, V * PACK], BF16, name=f"grouped{a}", tag=f"grouped{a}", align_bytes=64)
             (nc.vector.tensor_copy if a == 0 else nc.scalar.copy)(
                 grouped[:].rearrange("p (b c m j) -> p c j m b", b=BLOCKS, m=2, j=PACK),
                 h_raw[a][:].rearrange("p j (c m b) -> p c j m b", m=2, b=BLOCKS),

@@ -48,13 +48,13 @@ def tile_picked_ymp2_reg_p_kernel(tc, x_words, x_scales, hT, eo, ev, offs, swp, 
             out=ident[:], in_=zeros[:], compare_op=ALU.not_equal, fill=1.0, base=0, pattern=[[-1, P]], channel_multiplier=1
         )
 
+        h_rows = hT.rearrange("(a p j) w -> a p j w", a=PASSES, j=PACK)
         nc.sync.dma_start(eo_col[:], eo[0:1, :].rearrange("o (p c) -> (o p) c", c=PACK))
         nc.sync.dma_start(ev_col[:], ev.rearrange("(p b) o -> p (b o)", b=BLOCKS))
         nc.sync.dma_start(offs_sb[:], offs)
+        nc.sync.dma_start(h_raw[0][:], h_rows[0])
+        nc.sync.dma_start(h_raw[1][:], h_rows[1])
         nc.sync.dma_start(swp_sb[:], swp)
-        h_rows = hT.rearrange("(a p j) w -> a p j w", a=PASSES, j=PACK)
-        for a in range(PASSES):
-            nc.sync.dma_start(h_raw[a][:], h_rows[a])
         for q in range(P // QUAD):
             nc.sync.dma_start(
                 scale_rows[:].bitcast(I32)[QUAD * q : QUAD * q + PACK * PASSES, :],
@@ -147,20 +147,20 @@ def tile_picked_ymp2_reg_p_kernel(tc, x_words, x_scales, hT, eo, ev, offs, swp, 
         yf = [[sb.tile([P, HALF], F32, name=f"yf{b}{h}") for h in range(2)] for b in range(BLOCKS)]
         for h in range(2):
             for b in range(BLOCKS):
-                if h == 1 and b == 1:
+                if h == 1 and b == 0:
                     nc.vector.tensor_copy(y_sb[b][:, HALF * h : HALF * (h + 1)], y_ps[b][h][:])
                 else:
                     nc.scalar.copy(y_sb[b][:, HALF * h : HALF * (h + 1)], y_ps[b][h][:])
             for b in range(BLOCKS):
-                nc.vector.tensor_tensor(yf[b][h][:], y_ps[b][h][:], neg_f[b][:, HALF * h : HALF * (h + 1)], ALU.mult)
+                nc.vector.tensor_tensor(yf[b][h][:], y_sb[b][:, HALF * h : HALF * (h + 1)], neg_f[b][:, HALF * h : HALF * (h + 1)], ALU.mult)
 
         out_rows = out.rearrange("(p b) n -> b p n", b=BLOCKS)
         for b in range(BLOCKS):
             for h in range(2):
                 yx = sb.tile([P, HALF], F32, name=f"yx{b}{h}")
                 nc.scalar.activation(yx[:], y_sb[b][:].indirect(swp_sb[:, cols * h : cols * (h + 1)]), ACT.Copy)
-                diff = sb.tile([P, HALF], F32, name=f"diff{b}{h}")
-                nc.vector.scalar_tensor_tensor(diff[:], y_ps[b][h][:], -2.0, yx[:], ALU.mult, ALU.add)
+                diff = sb.tile([P, HALF], F32, name=f"diff{b}{h}", tag="diff", bufs=2)
+                nc.vector.scalar_tensor_tensor(diff[:], y_sb[b][:, HALF * h : HALF * (h + 1)], -2.0, yx[:], ALU.mult, ALU.add)
                 res = sb.tile([P, HALF], F32, name=f"res{b}{h}")
                 nc.vector.tensor_tensor(res[:], diff[:], yf[b][h][:], ALU.mult)
                 nc.sync.dma_start(out_rows[b][:, HALF * h : HALF * (h + 1)], res[:])

@@ -89,9 +89,6 @@ def tile_picked_ymp2_reg_p_kernel(tc, x_words, x_scales, hT, eo, ev, offs, swp, 
             nc.scalar.activation(r[:], eo_ps[:].rearrange("p c n -> p n c"), ACT.Abs_reciprocal_sqrt, bias=ev_col[:, b : b + 1])
             rs.append(r)
 
-        picked_scales = sb.tile([P, S], U8, name="picked_scales", align_bytes=64)
-        nc.vector.tensor_copy(picked_scales[:], scale_rows[:].indirect(offs_sb[:]))
-
         ms = []
         for b in range(BLOCKS):
             m = sb.tile([P, P, PACK], F32, name=f"root{b}", tag=f"root{b}")
@@ -99,6 +96,9 @@ def tile_picked_ymp2_reg_p_kernel(tc, x_words, x_scales, hT, eo, ev, offs, swp, 
                 m[:], exp_ps[:].rearrange("p c n -> p n c"), inv_exp_ev[:, b : b + 1], rs[b][:], ALU.subtract, ALU.mult
             )
             ms.append(m)
+
+        picked_scales = sb.tile([P, S], U8, name="picked_scales", tag="rsq1", align_bytes=64)
+        nc.vector.tensor_copy(picked_scales[:], scale_rows[:].indirect(offs_sb[:]))
 
         h_codes, h_scales = [], []
         for a in range(PASSES):
@@ -133,13 +133,13 @@ def tile_picked_ymp2_reg_p_kernel(tc, x_words, x_scales, hT, eo, ev, offs, swp, 
                     stop=(a == PASSES - 1),
                 )
 
-        picked0 = sb.tile([P, S], U32, name="picked0", tag="rsq1", align_bytes=64)
+        picked0 = sb.tile([P, S], U32, name="picked0", tag="scales_then_picked", align_bytes=64)
         nc.vector.tensor_copy(picked0[:], words[0][:].indirect(offs_sb[:]))
         for h in range(2):
             product(0, h, picked0[:, HALF * h : HALF * (h + 1)])
         cols = HALF // LANES
         for h in range(2):
-            picked1 = sb.tile([P, HALF], U32, name=f"picked1{h}", tag=("scales_then_picked" if h == 0 else "picked_last"), align_bytes=64)
+            picked1 = sb.tile([P, HALF], U32, name=f"picked1{h}", align_bytes=64)
             nc.vector.tensor_copy(picked1[:], words[1][:].indirect(offs_sb[:, cols * h : cols * (h + 1)]))
             product(1, h, picked1[:])
 

from contextlib import ExitStack

import concourse.mybir as mybir

K, T, S, V = 1024, 2048, 512, 256
FLOPS = 2 * K * S * V
BYTES = K * T + K // 32 * T + 4 * K * V + 4 * S + 4 * V + 2 * 2 * 128 * (S // 16) + 4 * V * S

F32 = mybir.dt.float32
BF16 = mybir.dt.bfloat16
I32 = mybir.dt.int32
U32 = mybir.dt.uint32
U16 = mybir.dt.uint16
U8 = mybir.dt.uint8
FP8X4 = mybir.dt.float8_e4m3fn_x4
ALU = mybir.AluOpType
ACT = mybir.ActivationFunctionType

P = 128
PACK = 4
PASSES = K // (P * PACK)
BLOCKS = V // P
HALF = S // 2
LANES = 16
QUAD = 32
RATE = 0.7
EXP_FLOOR = 1e-18


def tile_picked_ymp2_reg_p_kernel(tc, x_words, x_scales, hT, eo, ev, offs, swp, out):
    nc = tc.nc
    with ExitStack() as ctx:
        sb = ctx.enter_context(tc.tile_pool(name="sb", bufs=1))
        ps = ctx.enter_context(tc.psum_pool(name="ps", bufs=1))

        offs_sb = sb.tile([P, S // LANES], U16, name="offs_sb")
        swp_sb = sb.tile([P, S // LANES], U16, name="swp_sb")
        eo_col = sb.tile([P, PACK], F32, name="eo_col", tag="eo_then_words")
        ev_col = sb.tile([P, BLOCKS], F32, name="ev_col", tag="grouped1", align_bytes=64)
        h_raw = [sb.tile([P, PACK, V], F32, name=f"h_raw{a}") for a in range(PASSES)]
        scale_rows = sb.tile([P, T], U8, name="scale_rows", tag="scales_then_picked", align_bytes=64)

        nc.gpsimd.memset(scale_rows[:].bitcast(I32), 0)
        zeros = sb.tile([P, P], F32, name="zeros", tag="zeros_then_words")
        nc.gpsimd.memset(zeros[:], 0.0)
        ident = sb.tile([P, P], F32, name="ident")
        nc.gpsimd.affine_select(
            out=ident[:], in_=zeros[:], compare_op=ALU.not_equal, fill=1.0, base=0, pattern=[[-1, P]], channel_multiplier=1
        )

        h_rows = hT.rearrange("(a p j) w -> a p j w", a=PASSES, j=PACK)
        nc.sync.dma_start(eo_col[:], eo[0:1, :].rearrange("o (p c) -> (o p) c", c=PACK))
        nc.sync.dma_start(ev_col[:], ev.rearrange("(p b) o -> p (b o)", b=BLOCKS))
        nc.sync.dma_start(offs_sb[:], offs)
        nc.sync.dma_start(h_raw[0][:], h_rows[0])
        nc.sync.dma_start(h_raw[1][:], h_rows[1])
        nc.sync.dma_start(swp_sb[:], swp)
        for q in range(P // QUAD):
            nc.sync.dma_start(
                scale_rows[:].bitcast(I32)[QUAD * q : QUAD * q + PACK * PASSES, :],
                x_scales.bitcast(I32)[:, PACK * q : PACK * (q + 1), :],
            )

        exp_eo = sb.tile([P, PACK], F32, name="exp_eo")
        nc.scalar.activation(exp_eo[:], eo_col[:], ACT.Exp, scale=RATE)
        exp_ev_raw = sb.tile([P, BLOCKS], F32, name="exp_ev_raw")
        nc.scalar.activation(exp_ev_raw[:], ev_col[:], ACT.Exp, scale=RATE)
        exp_ev = sb.tile([P, BLOCKS], F32, name="exp_ev")
        nc.vector.tensor_scalar_max(exp_ev[:], exp_ev_raw[:], EXP_FLOOR)
        inv_exp_ev = sb.tile([P, BLOCKS], F32, name="inv_exp_ev")
        nc.vector.reciprocal(inv_exp_ev[:], exp_ev[:])

        eo_ps = ps.tile([P, PACK, P], F32, name="eo_ps", tag="bank00")
        for c in range(PACK):
            nc.tensor.transpose(eo_ps[:, c, :], eo_col[:, c : c + 1].to_broadcast([P, P]), ident[:])
        exp_ps = ps.tile([P, PACK, P], F32, name="exp_ps", tag="bank10")
        for c in range(PACK):
            nc.tensor.transpose(exp_ps[:, c, :], exp_eo[:, c : c + 1].to_broadcast([P, P]), ident[:])

        words = []
        for a, tag in enumerate(("zeros_then_words", "eo_then_words")):
            w = sb.tile([P, T], U32, name=f"words{a}", tag=tag)
            nc.sync.dma_start(w[:].bitcast(I32), x_words[a].rearrange("p n t -> p (n t)").bitcast(I32))
            words.append(w)

        rs = []
        for b in range(BLOCKS):
            r = sb.tile([P, P, PACK], F32, name=f"rsq{b}", tag=f"rsq{b}", align_bytes=64)
            nc.scalar.activation(r[:], eo_ps[:].rearrange("p c n -> p n c"), ACT.Abs_reciprocal_sqrt, bias=ev_col[:, b : b + 1])
            rs.append(r)

        ms = []
        for b in range(BLOCKS):
            m = sb.tile([P, P, PACK], F32, name=f"root{b}", tag=f"root{b}")
            nc.vector.scalar_tensor_tensor(
                m[:], exp_ps[:].rearrange("p c n -> p n c"), inv_exp_ev[:, b : b + 1], rs[b][:], ALU.subtract, ALU.mult
            )
            ms.append(m)

        picked_scales = sb.tile([P, S], U8, name="picked_scales", tag="rsq1", align_bytes=64)
        nc.vector.tensor_copy(picked_scales[:], scale_rows[:].indirect(offs_sb[:]))

        h_codes, h_scales = [], []
        for a in range(PASSES):
            grouped = sb.tile([P, V * PACK], BF16, name=f"grouped{a}", tag=f"grouped{a}", align_bytes=64)
            (nc.vector.tensor_copy if a == 0 else nc.scalar.copy)(
                grouped[:].rearrange("p (b c m j) -> p c j m b", b=BLOCKS, m=2, j=PACK),
                h_raw[a][:].rearrange("p j (c m b) -> p c j m b", m=2, b=BLOCKS),
            )
            codes = sb.tile([P, V], U32, name=f"h_codes{a}", align_bytes=64)
            scales = sb.tile([P, V], U8, name=f"h_scales{a}", align_bytes=64)
            nc.vector.quantize_mx(out=codes[:].bitcast(FP8X4), scales=scales[:], in_=grouped[:])
            h_codes.append(codes)
            h_scales.append(scales)

        neg_f = []
        for b in range(BLOCKS):
            f = sb.tile([P, S], F32, name=f"neg_f{b}")
            nc.scalar.activation(f[:], ms[b][:].rearrange("p n c -> p (n c)"), ACT.Square, scale=exp_ev[:, b : b + 1])
            neg_f.append(f)

        y_ps = [[ps.tile([P, HALF], F32, name=f"y_ps{b}{h}", tag=f"bank{b}{h}") for h in range(2)] for b in range(BLOCKS)]

        def product(a, h, picked):
            for b in range(BLOCKS):
                nc.tensor.matmul_mx(
                    out=y_ps[b][h][:],
                    lhsT=h_codes[a][:, P * b : P * (b + 1)].bitcast(FP8X4),
                    lhsT_scale=h_scales[a][:, P * b : P * (b + 1)],
                    rhs=picked.bitcast(FP8X4),
                    rhs_scale=picked_scales[PACK * a :, HALF * h : HALF * (h + 1)],
                    start=(a == 0),
                    stop=(a == PASSES - 1),
                )

        picked0 = sb.tile([P, S], U32, name="picked0", tag="scales_then_picked", align_bytes=64)
        nc.vector.tensor_copy(picked0[:], words[0][:].indirect(offs_sb[:]))
        for h in range(2):
            product(0, h, picked0[:, HALF * h : HALF * (h + 1)])
        cols = HALF // LANES
        for h in range(2):
            picked1 = sb.tile([P, HALF], U32, name=f"picked1{h}", align_bytes=64)
            nc.vector.tensor_copy(picked1[:], words[1][:].indirect(offs_sb[:, cols * h : cols * (h + 1)]))
            product(1, h, picked1[:])

        y_sb = [sb.tile([P, S], F32, name=f"y_sb{b}", tag=f"root{1 - b}") for b in range(BLOCKS)]
        yf = [[sb.tile([P, HALF], F32, name=f"yf{b}{h}") for h in range(2)] for b in range(BLOCKS)]
        for h in range(2):
            for b in range(BLOCKS):
                if h == 1 and b == 0:
                    nc.vector.tensor_copy(y_sb[b][:, HALF * h : HALF * (h + 1)], y_ps[b][h][:])
                else:
                    nc.scalar.copy(y_sb[b][:, HALF * h : HALF * (h + 1)], y_ps[b][h][:])
            for b in range(BLOCKS):
                nc.vector.tensor_tensor(yf[b][h][:], y_sb[b][:, HALF * h : HALF * (h + 1)], neg_f[b][:, HALF * h : HALF * (h + 1)], ALU.mult)

        out_rows = out.rearrange("(p b) n -> b p n", b=BLOCKS)
        for b in range(BLOCKS):
            for h in range(2):
                yx = sb.tile([P, HALF], F32, name=f"yx{b}{h}")
                nc.scalar.activation(yx[:], y_sb[b][:].indirect(swp_sb[:, cols * h : cols * (h + 1)]), ACT.Copy)
                diff = sb.tile([P, HALF], F32, name=f"diff{b}{h}", tag="diff", bufs=2)
                nc.vector.scalar_tensor_tensor(diff[:], y_sb[b][:, HALF * h : HALF * (h + 1)], -2.0, yx[:], ALU.mult, ALU.add)
                res = sb.tile([P, HALF], F32, name=f"res{b}{h}")
                nc.vector.tensor_tensor(res[:], diff[:], yf[b][h][:], ALU.mult)
                nc.sync.dma_start(out_rows[b][:, HALF * h : HALF * (h + 1)], res[:])
